import numpy as np
import ml_dtypes


def mxq(x, axis, fmt="e4m3"):
    dtype, down = {"e4m3": (ml_dtypes.float8_e4m3fn, 7), "e5m2": (ml_dtypes.float8_e5m2, 14)}[fmt]
    v = np.moveaxis(np.asarray(x, np.float32).astype(ml_dtypes.bfloat16).astype(np.float64), axis, -1)
    blocks = v.reshape(v.shape[:-1] + (-1, 32))
    amax = np.abs(blocks).max(-1, keepdims=True)
    byte = np.maximum(np.where(amax > 0, np.frexp(amax)[1] - 1 + 127, 0) - down, 1)
    scale = np.exp2(byte - 127.0)
    codes = (blocks / scale).astype(np.float32).astype(dtype).astype(np.float64)
    return np.moveaxis((codes * scale).reshape(v.shape), -1, axis)


WIDE = False


def mx_kscale(k):
    if not WIDE:
        return np.ones(k)
    levels = np.array([10, -10, 5, -5, 0])
    if k % 512:
        return np.exp2(np.random.permutation(np.resize(levels, k // 32))).repeat(32)
    a = np.empty((k // 512, 16))
    for p in range(k // 512):
        a[p, :8] = np.random.permutation(np.resize(levels, 8))
        for g in range(8):
            far = levels[np.abs(levels - a[p, g]) >= 10]
            a[p, g + 8] = far[np.random.randint(len(far))]
    return np.exp2(a.ravel()).repeat(32)


def f64(x):
    return np.asarray(x).astype(np.float64)


def striped(idx):
    return np.tile(idx.reshape(-1, 16).T, (8, 1)).astype(np.uint16)


def unstriped(offs):
    return offs[:16].T.reshape(-1).astype(np.int64)


def striped8(idx):
    return np.concatenate([x.reshape(-1, 16).T for x in idx]).astype(np.uint16)


def runs(offs, k):
    lists = np.stack([offs[16 * r : 16 * r + 16].T.reshape(-1) for r in range(8)]).astype(np.int64)
    return lists[np.arange(k) % 512 // 64]


def pack_weight(w):
    k, n = w.shape
    w = f64(np.asarray(w, np.float32).astype(ml_dtypes.bfloat16)).reshape(k // 32, 32, n)
    amax = np.abs(w).max(1)
    byte = np.clip(np.where(amax > 0, np.frexp(amax)[1] - 1 + 127 - 7, 1), 1, 254)
    scaled = (w * np.exp2(127.0 - byte)[:, None, :]).reshape(k, n).astype(np.float32)
    words = np.ascontiguousarray(scaled.reshape(k // 512, 128, 4, n).transpose(0, 1, 3, 2)).astype(ml_dtypes.float8_e4m3fn).view(np.uint8)
    return words, np.ascontiguousarray(byte.astype(np.uint8).reshape(k // 512, 16, n))


def unpack_weight(words, scales):
    g, p, n, _ = words.shape
    vals = np.ascontiguousarray(words).view(ml_dtypes.float8_e4m3fn).astype(np.float64) * np.repeat(np.exp2(scales.astype(np.float64) - 127.0), 8, axis=1)[..., None]
    return vals.transpose(0, 1, 3, 2).reshape(g * 512, n)


E2M1 = np.array([0.0, 0.5, 1.0, 1.5, 2.0, 3.0, 4.0, 6.0, -0.0, -0.5, -1.0, -1.5, -2.0, -3.0, -4.0, -6.0])


def pack_fp4(w):
    k, n = w.shape
    w = f64(np.asarray(w, np.float32).astype(ml_dtypes.bfloat16)).reshape(k // 32, 32, n)
    amax = np.abs(w).max(1)
    mant, ex = np.frexp(amax / 6.0)
    byte = np.clip(np.where(amax > 0, np.where(mant > 0.5, ex, ex - 1) + 127, 1), 1, 254)
    scaled = (w * np.exp2(127.0 - byte)[:, None, :]).reshape(k, n).astype(np.float32)
    c = np.ascontiguousarray(scaled.reshape(k // 512, 128, 4, n).transpose(0, 1, 3, 2)).astype(ml_dtypes.float4_e2m1fn).view(np.uint8) & 0xF
    words = (c[..., 0::2] | (c[..., 1::2] << 4)).reshape(k // 512, 128, 2 * n)
    return np.ascontiguousarray(words), np.ascontiguousarray(byte.astype(np.uint8).reshape(k // 512, 16, n))


def unpack_fp4(words, scales):
    g, _, n = scales.shape
    words = np.ascontiguousarray(words).reshape(g, 128, n, 2)
    nib = np.empty((g, 128, n, 4), np.uint8)
    nib[..., 0::2] = words & 0xF
    nib[..., 1::2] = words >> 4
    vals = E2M1[nib] * np.repeat(np.exp2(scales.astype(np.float64) - 127.0), 8, axis=1)[..., None]
    return vals.transpose(0, 1, 3, 2).reshape(g * 512, n)


K, T, S, H, G, U = 512, 2048, 256, 512, 2048, 512


def setup_inputs():
    n = np.random.standard_normal
    s = mx_kscale(K)[:, None]
    packed_xT = pack_weight(n((K, T)) * s)
    packed_w1 = pack_fp4(n((K, H)) / np.sqrt(K) / s)
    packed_dT = pack_weight(n((K, G)) / s)
    perm = np.random.permutation(U)
    return {
        "x_words": packed_xT[0],
        "x_scales": packed_xT[1],
        "w1_words": packed_w1[0],
        "w1_scales": packed_w1[1],
        "gs": (np.random.uniform(0.5, 1.5, (K, 1)) * s).astype(np.float32),
        "d_words": packed_dT[0],
        "d_scales": packed_dT[1],
        "offs": striped8(np.random.randint(0, T, (8, S))),
        "n1": striped(np.random.permutation(S)),
        "ka": striped8(np.random.randint(0, G, (8, H))),
        "kb": striped8(np.random.randint(0, G, (8, H))),
        "n2": striped(perm[:S]),
        "n3": striped(perm[S:]),
        "n4": striped(np.random.permutation(S)),
    }


def reference(x_words, x_scales, w1_words, w1_scales, gs, d_words, d_scales, offs, n1, ka, kb, n2, n3, n4):
    d_ka = unpack_weight(d_words, d_scales)[np.arange(K)[:, None], runs(ka, K)]
    xq = unpack_weight(x_words, x_scales)[np.arange(K)[:, None], runs(offs, K)]
    y = unpack_fp4(w1_words, w1_scales).T @ xq
    ds = np.zeros((H, S))
    ds[:, unstriped(n1)] = y
    z = f64(gs) * (y - ds)
    zq = mxq(z, 0, "e4m3")
    d_kb = unpack_weight(d_words, d_scales)[np.arange(K)[:, None], runs(kb, K)]
    h = 0.0625 * (d_ka.T @ zq + d_kb.T @ zq)
    dn = np.minimum(h, h[:, unstriped(n4)])
    up = np.maximum(h, h[:, unstriped(n4)])
    ph = np.zeros((H, U))
    ph[:, unstriped(n2)] = up
    out = ph.copy()
    out[:, unstriped(n3)] = dn
    return out

@@ -1,0 +1,177 @@
+from contextlib import ExitStack
+
+import concourse.mybir as mybir
+
+F32 = mybir.dt.float32
+BF16 = mybir.dt.bfloat16
+U32 = mybir.dt.uint32
+I32 = mybir.dt.int32
+U16 = mybir.dt.uint16
+U8 = mybir.dt.uint8
+FP8X4 = mybir.dt.float8_e4m3fn_x4
+FP4X4 = mybir.dt.float4_e2m1fn_x4
+ALU = mybir.AluOpType
+COPY = mybir.ActivationFunctionType.Copy
+
+P = 128
+K, T, S, H, G, U = 512, 2048, 256, 512, 2048, 512
+PACK = 4
+HALF = S // 2
+H_WINDOW = S + 16
+FLOPS = 2 * K * H * S * 3
+
+
+def tile_picked_hdaqsendmxpagmx_none_p_kernel(
+    tc, x_words, x_scales, w1_words, w1_scales, gs, d_words, d_scales, offs, n1, ka, kb, n2, n3, n4, out
+):
+    nc = tc.nc
+    with ExitStack() as ctx:
+        keep = ctx.enter_context(tc.tile_pool(name="keep", bufs=1))
+        psum = ctx.enter_context(tc.psum_pool(name="psum", bufs=1))
+
+        def load_list(src, name):
+            lst = keep.tile(list(src.shape), U16, name=name)
+            nc.sync.dma_start(lst[:], src)
+            return lst
+
+        def load_scale_rows(engine, clear, src, name):
+            window = keep.tile([P, T], U8, name=name)
+            clear.memset(window[:].bitcast(I32), 0)
+            rows = src[0].bitcast(I32)
+            for j in range(2):
+                engine.dma_start(window[:].bitcast(I32)[j:P:16, :], rows[j:16:2, :])
+            return window
+
+        def place_scale_rows(engine, picked, name):
+            plane = keep.tile(list(picked.shape), U8, name=name, align_bytes=64)
+            nc.vector.tensor_copy(plane[:].bitcast(I32), picked[:].bitcast(I32))
+            for j in range(2):
+                engine.dma_start(plane[:].bitcast(I32)[2 + j:P:32, :], picked[:].bitcast(I32)[16 + j:P:32, :])
+            return plane
+
+        def load_words(src, name):
+            window = keep.tile([P, T], U32, name=name)
+            nc.sync.dma_start(window[:].bitcast(I32), src[0].rearrange("p c r -> p (c r)").bitcast(I32))
+            return window
+
+        offs_t = load_list(offs, "offs_t")
+        xs_win = load_scale_rows(nc.scalar, nc.vector, x_scales, "xs_win")
+        xw_win = load_words(x_words, "xw_win")
+
+        w1w_raw = keep.tile([P, 2 * H], U8)
+        nc.scalar.dma_start(w1w_raw[:].bitcast(I32), w1_words[0].bitcast(I32))
+        w1s_raw = keep.tile([P, H], U8)
+        nc.vector.memset(w1s_raw[:].bitcast(I32), 0)
+        for j in range(4):
+            nc.scalar.dma_start(w1s_raw[:].bitcast(I32)[j:P:32, :], w1_scales[0].bitcast(I32)[j:16:4, :])
+
+        xs_picked = keep.tile([P, S], U8)
+        nc.vector.tensor_copy(xs_picked[:], xs_win[:].indirect(offs_t[:]))
+        xs_plane = place_scale_rows(nc.scalar, xs_picked, "xs_plane")
+
+        w1w = keep.tile([P, 2 * H], U8, align_bytes=64)
+        nc.scalar.copy(
+            w1w[:].bitcast(U16).rearrange("p (t m) -> p t m", t=PACK),
+            w1w_raw[:].bitcast(U16).rearrange("p (m t) -> p t m", t=PACK),
+        )
+        w1s = keep.tile([P, H], U8, align_bytes=64)
+        nc.vector.tensor_copy(
+            w1s[:].rearrange("p (t m) -> p t m", t=PACK), w1s_raw[:].rearrange("p (m t) -> p t m", t=PACK)
+        )
+        xw = keep.tile([P, S], U32, align_bytes=64)
+        nc.vector.tensor_copy(xw[:], xw_win[:].indirect(offs_t[:]))
+
+        gs_t = keep.tile([P, PACK], F32)
+        nc.gpsimd.dma_start(gs_t[:], gs.rearrange("(p t) o -> p (t o)", t=PACK))
+        n1_t = load_list(n1, "n1_t")
+        ka_t = load_list(ka, "ka_t")
+        kb_t = load_list(kb, "kb_t")
+        ds_win = load_scale_rows(nc.gpsimd, nc.gpsimd, d_scales, "ds_win")
+        dw_win = load_words(d_words, "dw_win")
+
+        z = keep.tile([P, S, PACK], BF16, align_bytes=64)
+        gy, gds = [], []
+        for t in range(PACK):
+            y_ps = psum.tile([P, S], F32, name=f"y_ps{t}")
+            nc.tensor.matmul_mx(
+                y_ps[:], w1w[:, 2 * P * t:2 * P * (t + 1)].bitcast(FP4X4), w1s[:, P * t:P * (t + 1)],
+                xw[:].bitcast(FP8X4), xs_plane[:], start=True, stop=True,
+            )
+            gy_t = keep.tile([P, S], F32, name=f"gy{t}")
+            if t == 0:
+                nc.scalar.activation(gy_t[:], y_ps[:], COPY, scale=gs_t[:, t:t + 1])
+            else:
+                nc.vector.tensor_scalar(gy_t[:], y_ps[:], gs_t[:, t:t + 1], None, ALU.mult)
+            gds_t = keep.tile([P, 2 * S], F32, name=f"gds{t}")
+            nc.scalar.activation(gds_t[:].indirect(n1_t[:]), gy_t[:], COPY)
+            gy.append(gy_t)
+            gds.append(gds_t)
+
+        ds_picked = keep.tile([P, 2 * H], U8)
+        for u, lst in enumerate((ka_t, kb_t)):
+            nc.vector.tensor_copy(ds_picked[:, u * H:(u + 1) * H], ds_win[:].indirect(lst[:]))
+        ds_plane = place_scale_rows(nc.sync, ds_picked, "ds_plane")
+
+        def pick_d_words(half):
+            picked = []
+            for u, lst in enumerate((ka_t, kb_t)):
+                words = keep.tile([P, S], U32, name=f"dw{u}_{half}", align_bytes=64)
+                nc.vector.tensor_copy(words[:], dw_win[:].indirect(lst[:, 16 * half:16 * (half + 1)]))
+                picked.append(words)
+            return picked
+
+        nc.vector.tensor_tensor(z[:, :, 0], gy[0][:], gds[0][:, :S], ALU.subtract)
+        dw = [pick_d_words(0)]
+        for t in (1, 2):
+            nc.vector.tensor_tensor(z[:, :, t], gy[t][:], gds[t][:, :S], ALU.subtract)
+        halves = [slice(0, HALF), slice(HALF, S)]
+        for cols in halves:
+            nc.vector.tensor_tensor(z[:, cols, 3], gy[3][:, cols], gds[3][:, cols], ALU.subtract)
+        zw = keep.tile([P, S], U32, align_bytes=64)
+        zs = keep.tile([P, S], U8, align_bytes=64)
+        for cols in halves:
+            nc.vector.quantize_mx(zw[:, cols].bitcast(FP8X4), zs[:, cols], z[:, cols, :].rearrange("p c t -> p (c t)"))
+
+        n4_t = load_list(n4, "n4_t")
+        n2_t = load_list(n2, "n2_t")
+        n3_t = load_list(n3, "n3_t")
+
+        def product(m):
+            h_ps = psum.tile([P, S], F32, name=f"h_ps{m}")
+            for cols in halves if m == 0 else [slice(0, S)]:
+                for u in range(2):
+                    rows = slice((m % 2) * P, (m % 2 + 1) * P)
+                    nc.tensor.matmul_mx(
+                        h_ps[:, cols], dw[m // 2][u][:, rows].bitcast(FP8X4),
+                        ds_plane[:, u * H + m * P:u * H + (m + 1) * P],
+                        zw[:, cols].bitcast(FP8X4), zs[:, cols], start=(u == 0), stop=(u == 1),
+                    )
+            h = keep.tile([P, H_WINDOW], F32, name=f"h{m}")
+            nc.gpsimd.memset(h[:, S:], 0.0)
+            if m == 0:
+                nc.scalar.activation(h[:, :S], h_ps[:], COPY, scale=0.0625)
+            else:
+                nc.vector.tensor_scalar(h[:, :S], h_ps[:], 0.0625, None, ALU.mult)
+            return h
+
+        def fetch(m, h):
+            other = keep.tile([P, S], F32, name=f"other{m}")
+            nc.scalar.activation(other[:], h[:].indirect(n4_t[:]), COPY)
+            up = keep.tile([P, S], F32, name=f"up{m}")
+            nc.vector.tensor_tensor(up[:], h[:, :S], other[:], ALU.max)
+            dn = keep.tile([P, S], F32, name=f"dn{m}")
+            nc.vector.tensor_tensor(dn[:], h[:, :S], other[:], ALU.min)
+            return up, dn
+
+        for pair in range(2):
+            if pair == 1:
+                dw.append(pick_d_words(1))
+            blocks = (2 * pair, 2 * pair + 1)
+            hs = [product(m) for m in blocks]
+            ups_dns = [fetch(m, h) for m, h in zip(blocks, hs)]
+            pages = [keep.tile([P, U], F32, name=f"page{m}") for m in blocks]
+            for page, (up, dn) in zip(pages, ups_dns):
+                nc.scalar.activation(page[:].indirect(n2_t[:]), up[:], COPY)
+            for m, page, (up, dn) in zip(blocks, pages, ups_dns):
+                nc.scalar.activation(page[:].indirect(n3_t[:]), dn[:], COPY)
+                nc.sync.dma_start(out[m * P:(m + 1) * P, :], page[:])

@@ -49,27 +49,27 @@ def tile_picked_hdaqsendmxpagmx_none_p_kernel(
                 engine.dma_start(plane[:].bitcast(I32)[2 + j:P:32, :], picked[:].bitcast(I32)[16 + j:P:32, :])
             return plane
 
-        def load_words(src, name):
+        def load_words(engine, src, name):
             window = keep.tile([P, T], U32, name=name)
-            nc.sync.dma_start(window[:].bitcast(I32), src[0].rearrange("p c r -> p (c r)").bitcast(I32))
+            engine.dma_start(window[:].bitcast(I32), src[0].rearrange("p c r -> p (c r)").bitcast(I32))
             return window
 
+        xw_win = load_words(nc.scalar, x_words, "xw_win")
         offs_t = load_list(offs, "offs_t")
-        xs_win = load_scale_rows(nc.scalar, nc.vector, x_scales, "xs_win")
-        xw_win = load_words(x_words, "xw_win")
+        xs_win = load_scale_rows(nc.sync, nc.vector, x_scales, "xs_win")
 
         w1w_raw = keep.tile([P, 2 * H], U8)
-        nc.scalar.dma_start(w1w_raw[:].bitcast(I32), w1_words[0].bitcast(I32))
+        nc.sync.dma_start(w1w_raw[:].bitcast(I32), w1_words[0].bitcast(I32))
         w1s_raw = keep.tile([P, H], U8)
         nc.vector.memset(w1s_raw[:].bitcast(I32), 0)
         for j in range(4):
-            nc.scalar.dma_start(w1s_raw[:].bitcast(I32)[j:P:32, :], w1_scales[0].bitcast(I32)[j:16:4, :])
+            nc.sync.dma_start(w1s_raw[:].bitcast(I32)[j:P:32, :], w1_scales[0].bitcast(I32)[j:16:4, :])
 
         xs_picked = keep.tile([P, S], U8)
         nc.vector.tensor_copy(xs_picked[:], xs_win[:].indirect(offs_t[:]))
         xs_plane = place_scale_rows(nc.scalar, xs_picked, "xs_plane")
 
-        w1w = keep.tile([P, 2 * H], U8, align_bytes=64)
+        w1w = keep.tile([P, 2 * H], U8, align_bytes=64, tag="w1w")
         nc.scalar.copy(
             w1w[:].bitcast(U16).rearrange("p (t m) -> p t m", t=PACK),
             w1w_raw[:].bitcast(U16).rearrange("p (m t) -> p t m", t=PACK),
@@ -78,7 +78,7 @@ def tile_picked_hdaqsendmxpagmx_none_p_kernel(
         nc.vector.tensor_copy(
             w1s[:].rearrange("p (t m) -> p t m", t=PACK), w1s_raw[:].rearrange("p (m t) -> p t m", t=PACK)
         )
-        xw = keep.tile([P, S], U32, align_bytes=64)
+        xw = keep.tile([P, S], U32, align_bytes=64, tag="xw")
         nc.vector.tensor_copy(xw[:], xw_win[:].indirect(offs_t[:]))
 
         gs_t = keep.tile([P, PACK], F32)
@@ -87,12 +87,12 @@ def tile_picked_hdaqsendmxpagmx_none_p_kernel(
         ka_t = load_list(ka, "ka_t")
         kb_t = load_list(kb, "kb_t")
         ds_win = load_scale_rows(nc.gpsimd, nc.gpsimd, d_scales, "ds_win")
-        dw_win = load_words(d_words, "dw_win")
+        dw_win = load_words(nc.sync, d_words, "dw_win")
 
-        z = keep.tile([P, S, PACK], BF16, align_bytes=64)
+        z = keep.tile([P, S, PACK], BF16, align_bytes=64, tag="z")
         gy, gds = [], []
         for t in range(PACK):
-            y_ps = psum.tile([P, S], F32, name=f"y_ps{t}")
+            y_ps = psum.tile([P, S], F32, name=f"y_ps{t}", tag=f"bank{t}")
             nc.tensor.matmul_mx(
                 y_ps[:], w1w[:, 2 * P * t:2 * P * (t + 1)].bitcast(FP4X4), w1s[:, P * t:P * (t + 1)],
                 xw[:].bitcast(FP8X4), xs_plane[:], start=True, stop=True,
@@ -107,23 +107,23 @@ def tile_picked_hdaqsendmxpagmx_none_p_kernel(
             gy.append(gy_t)
             gds.append(gds_t)
 
-        ds_picked = keep.tile([P, 2 * H], U8)
+        ds_picked = keep.tile([P, 2 * H], U8, align_bytes=64, tag="xw")
         for u, lst in enumerate((ka_t, kb_t)):
             nc.vector.tensor_copy(ds_picked[:, u * H:(u + 1) * H], ds_win[:].indirect(lst[:]))
         ds_plane = place_scale_rows(nc.sync, ds_picked, "ds_plane")
 
-        def pick_d_words(half):
-            picked = []
+        def pick_d_words(half, tag):
+            words = keep.tile([P, 2 * S], U32, name=f"dw{half}", align_bytes=64, tag=tag)
             for u, lst in enumerate((ka_t, kb_t)):
-                words = keep.tile([P, S], U32, name=f"dw{u}_{half}", align_bytes=64)
-                nc.vector.tensor_copy(words[:], dw_win[:].indirect(lst[:, 16 * half:16 * (half + 1)]))
-                picked.append(words)
-            return picked
+                nc.vector.tensor_copy(words[:, u * S:(u + 1) * S], dw_win[:].indirect(lst[:, 16 * half:16 * (half + 1)]))
+            return words
 
-        nc.vector.tensor_tensor(z[:, :, 0], gy[0][:], gds[0][:, :S], ALU.subtract)
-        dw = [pick_d_words(0)]
+        z_planes = keep.tile([P, PACK - 1, S], BF16)
+        nc.vector.tensor_tensor(z_planes[:, 0, :], gy[0][:], gds[0][:, :S], ALU.subtract)
+        dw = [pick_d_words(0, "w1w")]
         for t in (1, 2):
-            nc.vector.tensor_tensor(z[:, :, t], gy[t][:], gds[t][:, :S], ALU.subtract)
+            nc.vector.tensor_tensor(z_planes[:, t, :], gy[t][:], gds[t][:, :S], ALU.subtract)
+        nc.vector.tensor_copy(z[:, :, :PACK - 1], z_planes[:].rearrange("p t c -> p c t"))
         halves = [slice(0, HALF), slice(HALF, S)]
         for cols in halves:
             nc.vector.tensor_tensor(z[:, cols, 3], gy[3][:, cols], gds[3][:, cols], ALU.subtract)
@@ -137,21 +137,21 @@ def tile_picked_hdaqsendmxpagmx_none_p_kernel(
         n3_t = load_list(n3, "n3_t")
 
         def product(m):
-            h_ps = psum.tile([P, S], F32, name=f"h_ps{m}")
-            for cols in halves if m == 0 else [slice(0, S)]:
+            h = keep.tile([P, H_WINDOW], F32, name=f"h{m}")
+            nc.gpsimd.memset(h[:, S:], 0.0)
+            for i, cols in enumerate(halves if m == 0 else [slice(0, S)]):
+                h_ps = psum.tile([P, cols.stop - cols.start], F32, name=f"h_ps{m}_{i}", tag=f"bank{(PACK + m + i + (m > 0)) % 8}")
                 for u in range(2):
-                    rows = slice((m % 2) * P, (m % 2 + 1) * P)
+                    rows = slice(u * S + (m % 2) * P, u * S + (m % 2 + 1) * P)
                     nc.tensor.matmul_mx(
-                        h_ps[:, cols], dw[m // 2][u][:, rows].bitcast(FP8X4),
+                        h_ps[:], dw[m // 2][:, rows].bitcast(FP8X4),
                         ds_plane[:, u * H + m * P:u * H + (m + 1) * P],
                         zw[:, cols].bitcast(FP8X4), zs[:, cols], start=(u == 0), stop=(u == 1),
                     )
-            h = keep.tile([P, H_WINDOW], F32, name=f"h{m}")
-            nc.gpsimd.memset(h[:, S:], 0.0)
-            if m == 0:
-                nc.scalar.activation(h[:, :S], h_ps[:], COPY, scale=0.0625)
-            else:
-                nc.vector.tensor_scalar(h[:, :S], h_ps[:], 0.0625, None, ALU.mult)
+                if m == 0:
+                    nc.scalar.activation(h[:, cols], h_ps[:], COPY, scale=0.0625)
+                else:
+                    nc.vector.tensor_scalar(h[:, cols], h_ps[:], 0.0625, None, ALU.mult)
             return h
 
         def fetch(m, h):
@@ -165,7 +165,7 @@ def tile_picked_hdaqsendmxpagmx_none_p_kernel(
 
         for pair in range(2):
             if pair == 1:
-                dw.append(pick_d_words(1))
+                dw.append(pick_d_words(1, "z"))
             blocks = (2 * pair, 2 * pair + 1)
             hs = [product(m) for m in blocks]
             ups_dns = [fetch(m, h) for m, h in zip(blocks, hs)]

@@ -34,40 +34,39 @@ def tile_picked_hdaqsendmxpagmx_none_p_kernel(
             nc.sync.dma_start(lst[:], src)
             return lst
 
-        def load_scale_rows(engine, clear, src, name):
+        def load_scale_rows(queues, clear, src, name):
             window = keep.tile([P, T], U8, name=name)
             clear.memset(window[:].bitcast(I32), 0)
             rows = src[0].bitcast(I32)
             for j in range(2):
-                engine.dma_start(window[:].bitcast(I32)[j:P:16, :], rows[j:16:2, :])
+                queues[j].dma_start(window[:].bitcast(I32)[j:P:16, :], rows[j:16:2, :])
             return window
 
-        def place_scale_rows(engine, picked, name):
+        def place_scale_rows(queues, picked, name):
             plane = keep.tile(list(picked.shape), U8, name=name, align_bytes=64)
             nc.vector.tensor_copy(plane[:].bitcast(I32), picked[:].bitcast(I32))
             for j in range(2):
-                engine.dma_start(plane[:].bitcast(I32)[2 + j:P:32, :], picked[:].bitcast(I32)[16 + j:P:32, :])
+                queues[j].dma_start(plane[:].bitcast(I32)[2 + j:P:32, :], picked[:].bitcast(I32)[16 + j:P:32, :])
             return plane
 
-        def load_words(engine, src, name):
-            window = keep.tile([P, T], U32, name=name)
-            engine.dma_start(window[:].bitcast(I32), src[0].rearrange("p c r -> p (c r)").bitcast(I32))
+        def load_words(src, name):
+            window = keep.tile([P, T], U32, name=name, tag=name, align_bytes=64)
+            nc.sync.dma_start(window[:].bitcast(I32), src[0].rearrange("p c r -> p (c r)").bitcast(I32))
             return window
 
-        xw_win = load_words(nc.scalar, x_words, "xw_win")
         offs_t = load_list(offs, "offs_t")
-        xs_win = load_scale_rows(nc.sync, nc.vector, x_scales, "xs_win")
-
         w1w_raw = keep.tile([P, 2 * H], U8)
-        nc.sync.dma_start(w1w_raw[:].bitcast(I32), w1_words[0].bitcast(I32))
+        nc.scalar.dma_start(w1w_raw[:].bitcast(I32), w1_words[0].bitcast(I32))
+        xs_win = load_scale_rows((nc.sync, nc.scalar), nc.gpsimd, x_scales, "xs_win")
         w1s_raw = keep.tile([P, H], U8)
         nc.vector.memset(w1s_raw[:].bitcast(I32), 0)
-        for j in range(4):
-            nc.sync.dma_start(w1s_raw[:].bitcast(I32)[j:P:32, :], w1_scales[0].bitcast(I32)[j:16:4, :])
+        for j, queue in enumerate((nc.sync, nc.scalar, nc.scalar, nc.scalar)):
+            queue.dma_start(w1s_raw[:].bitcast(I32)[j:P:32, :], w1_scales[0].bitcast(I32)[j:16:4, :])
+        xw_win = load_words(x_words, "xw_win")
 
         xs_picked = keep.tile([P, S], U8)
         nc.vector.tensor_copy(xs_picked[:], xs_win[:].indirect(offs_t[:]))
-        xs_plane = place_scale_rows(nc.scalar, xs_picked, "xs_plane")
+        xs_plane = place_scale_rows((nc.sync, nc.scalar), xs_picked, "xs_plane")
 
         w1w = keep.tile([P, 2 * H], U8, align_bytes=64, tag="w1w")
         nc.scalar.copy(
@@ -86,10 +85,9 @@ def tile_picked_hdaqsendmxpagmx_none_p_kernel(
         n1_t = load_list(n1, "n1_t")
         ka_t = load_list(ka, "ka_t")
         kb_t = load_list(kb, "kb_t")
-        ds_win = load_scale_rows(nc.gpsimd, nc.gpsimd, d_scales, "ds_win")
-        dw_win = load_words(nc.sync, d_words, "dw_win")
+        ds_win = load_scale_rows((nc.gpsimd, nc.gpsimd), nc.vector, d_scales, "ds_win")
+        dw_win = load_words(d_words, "dw_win")
 
-        z = keep.tile([P, S, PACK], BF16, align_bytes=64, tag="z")
         gy, gds = [], []
         for t in range(PACK):
             y_ps = psum.tile([P, S], F32, name=f"y_ps{t}", tag=f"bank{t}")
@@ -107,30 +105,30 @@ def tile_picked_hdaqsendmxpagmx_none_p_kernel(
             gy.append(gy_t)
             gds.append(gds_t)
 
-        ds_picked = keep.tile([P, 2 * H], U8, align_bytes=64, tag="xw")
-        for u, lst in enumerate((ka_t, kb_t)):
-            nc.vector.tensor_copy(ds_picked[:, u * H:(u + 1) * H], ds_win[:].indirect(lst[:]))
-        ds_plane = place_scale_rows(nc.sync, ds_picked, "ds_plane")
-
-        def pick_d_words(half, tag):
-            words = keep.tile([P, 2 * S], U32, name=f"dw{half}", align_bytes=64, tag=tag)
+        def pick_d_scales(pair, tag):
+            picked = keep.tile([P, 2 * S], U8, name=f"ds_picked{pair}", align_bytes=64, tag=tag)
             for u, lst in enumerate((ka_t, kb_t)):
-                nc.vector.tensor_copy(words[:, u * S:(u + 1) * S], dw_win[:].indirect(lst[:, 16 * half:16 * (half + 1)]))
-            return words
+                nc.vector.tensor_copy(picked[:, u * S:(u + 1) * S], ds_win[:].indirect(lst[:, 16 * pair:16 * (pair + 1)]))
+            return place_scale_rows((nc.sync, nc.sync), picked, f"ds_plane{pair}")
 
-        z_planes = keep.tile([P, PACK - 1, S], BF16)
-        nc.vector.tensor_tensor(z_planes[:, 0, :], gy[0][:], gds[0][:, :S], ALU.subtract)
-        dw = [pick_d_words(0, "w1w")]
-        for t in (1, 2):
+        ds_planes = [pick_d_scales(0, "xw")]
+        dw = keep.tile([P, 2 * H], U32, align_bytes=64, tag="w1w")
+        for u, lst in enumerate((ka_t, kb_t)):
+            nc.vector.tensor_copy(dw[:, u * H:(u + 1) * H], dw_win[:].indirect(lst[:]))
+
+        z_store = keep.tile([P, (2 * PACK - 1) * S], BF16, align_bytes=64, tag="dw_win")
+        z = z_store[:, :PACK * S].rearrange("p (c t) -> p c t", t=PACK)
+        z_planes = z_store[:, PACK * S:].rearrange("p (t c) -> p t c", c=S)
+        for t in range(PACK - 1):
             nc.vector.tensor_tensor(z_planes[:, t, :], gy[t][:], gds[t][:, :S], ALU.subtract)
-        nc.vector.tensor_copy(z[:, :, :PACK - 1], z_planes[:].rearrange("p t c -> p c t"))
+        nc.vector.tensor_copy(z[:, :, :PACK - 1], z_planes.rearrange("p t c -> p c t"))
         halves = [slice(0, HALF), slice(HALF, S)]
         for cols in halves:
             nc.vector.tensor_tensor(z[:, cols, 3], gy[3][:, cols], gds[3][:, cols], ALU.subtract)
         zw = keep.tile([P, S], U32, align_bytes=64)
         zs = keep.tile([P, S], U8, align_bytes=64)
         for cols in halves:
-            nc.vector.quantize_mx(zw[:, cols].bitcast(FP8X4), zs[:, cols], z[:, cols, :].rearrange("p c t -> p (c t)"))
+            nc.vector.quantize_mx(zw[:, cols].bitcast(FP8X4), zs[:, cols], z_store[:, PACK * cols.start:PACK * cols.stop])
 
         n4_t = load_list(n4, "n4_t")
         n2_t = load_list(n2, "n2_t")
@@ -138,14 +136,13 @@ def tile_picked_hdaqsendmxpagmx_none_p_kernel(
 
         def product(m):
             h = keep.tile([P, H_WINDOW], F32, name=f"h{m}")
-            nc.gpsimd.memset(h[:, S:], 0.0)
+            nc.vector.memset(h[:, S:], 0.0)
             for i, cols in enumerate(halves if m == 0 else [slice(0, S)]):
                 h_ps = psum.tile([P, cols.stop - cols.start], F32, name=f"h_ps{m}_{i}", tag=f"bank{(PACK + m + i + (m > 0)) % 8}")
                 for u in range(2):
-                    rows = slice(u * S + (m % 2) * P, u * S + (m % 2 + 1) * P)
                     nc.tensor.matmul_mx(
-                        h_ps[:], dw[m // 2][:, rows].bitcast(FP8X4),
-                        ds_plane[:, u * H + m * P:u * H + (m + 1) * P],
+                        h_ps[:], dw[:, u * H + m * P:u * H + (m + 1) * P].bitcast(FP8X4),
+                        ds_planes[m // 2][:, u * S + (m % 2) * P:u * S + (m % 2 + 1) * P],
                         zw[:, cols].bitcast(FP8X4), zs[:, cols], start=(u == 0), stop=(u == 1),
                     )
                 if m == 0:
@@ -154,24 +151,22 @@ def tile_picked_hdaqsendmxpagmx_none_p_kernel(
                     nc.vector.tensor_scalar(h[:, cols], h_ps[:], 0.0625, None, ALU.mult)
             return h
 
-        def fetch(m, h):
-            other = keep.tile([P, S], F32, name=f"other{m}")
-            nc.scalar.activation(other[:], h[:].indirect(n4_t[:]), COPY)
-            up = keep.tile([P, S], F32, name=f"up{m}")
-            nc.vector.tensor_tensor(up[:], h[:, :S], other[:], ALU.max)
-            dn = keep.tile([P, S], F32, name=f"dn{m}")
-            nc.vector.tensor_tensor(dn[:], h[:, :S], other[:], ALU.min)
-            return up, dn
+        def combine(m, h, other, op):
+            res = keep.tile([P, S], F32, name=f"res{m}")
+            nc.vector.tensor_tensor(res[:], h[:, :S], other[:], op)
+            return res
 
         for pair in range(2):
             if pair == 1:
-                dw.append(pick_d_words(1, "z"))
+                ds_planes.append(pick_d_scales(1, "dw_win"))
             blocks = (2 * pair, 2 * pair + 1)
             hs = [product(m) for m in blocks]
-            ups_dns = [fetch(m, h) for m, h in zip(blocks, hs)]
+            others = [keep.tile([P, S], F32, name=f"other{m}") for m in blocks]
             pages = [keep.tile([P, U], F32, name=f"page{m}") for m in blocks]
-            for page, (up, dn) in zip(pages, ups_dns):
-                nc.scalar.activation(page[:].indirect(n2_t[:]), up[:], COPY)
-            for m, page, (up, dn) in zip(blocks, pages, ups_dns):
-                nc.scalar.activation(page[:].indirect(n3_t[:]), dn[:], COPY)
+            for h, other in zip(hs, others):
+                nc.scalar.activation(other[:], h[:].indirect(n4_t[:]), COPY)
+            for op, lst in ((ALU.max, n2_t), (ALU.min, n3_t)):
+                for m, h, other, page in zip(blocks, hs, others, pages):
+                    nc.scalar.activation(page[:].indirect(lst[:]), combine(m, h, other, op)[:], COPY)
+            for m, page in zip(blocks, pages):
                 nc.sync.dma_start(out[m * P:(m + 1) * P, :], page[:])

@@ -42,11 +42,11 @@ def tile_picked_hdaqsendmxpagmx_none_p_kernel(
                 queues[j].dma_start(window[:].bitcast(I32)[j:P:16, :], rows[j:16:2, :])
             return window
 
-        def place_scale_rows(queues, picked, name):
+        def place_scale_rows(picked, name):
             plane = keep.tile(list(picked.shape), U8, name=name, align_bytes=64)
             nc.vector.tensor_copy(plane[:].bitcast(I32), picked[:].bitcast(I32))
             for j in range(2):
-                queues[j].dma_start(plane[:].bitcast(I32)[2 + j:P:32, :], picked[:].bitcast(I32)[16 + j:P:32, :])
+                nc.sync.dma_start(plane[:].bitcast(I32)[2 + j:P:32, :], picked[:].bitcast(I32)[16 + j:P:32, :])
             return plane
 
         def load_words(src, name):
@@ -66,7 +66,7 @@ def tile_picked_hdaqsendmxpagmx_none_p_kernel(
 
         xs_picked = keep.tile([P, S], U8)
         nc.vector.tensor_copy(xs_picked[:], xs_win[:].indirect(offs_t[:]))
-        xs_plane = place_scale_rows((nc.sync, nc.scalar), xs_picked, "xs_plane")
+        xs_plane = place_scale_rows(xs_picked, "xs_plane")
 
         w1w = keep.tile([P, 2 * H], U8, align_bytes=64, tag="w1w")
         nc.scalar.copy(
@@ -81,7 +81,7 @@ def tile_picked_hdaqsendmxpagmx_none_p_kernel(
         nc.vector.tensor_copy(xw[:], xw_win[:].indirect(offs_t[:]))
 
         gs_t = keep.tile([P, PACK], F32)
-        nc.gpsimd.dma_start(gs_t[:], gs.rearrange("(p t) o -> p (t o)", t=PACK))
+        nc.sync.dma_start(gs_t[:], gs.rearrange("(p t) o -> p (t o)", t=PACK))
         n1_t = load_list(n1, "n1_t")
         ka_t = load_list(ka, "ka_t")
         kb_t = load_list(kb, "kb_t")
@@ -109,7 +109,7 @@ def tile_picked_hdaqsendmxpagmx_none_p_kernel(
             picked = keep.tile([P, 2 * S], U8, name=f"ds_picked{pair}", align_bytes=64, tag=tag)
             for u, lst in enumerate((ka_t, kb_t)):
                 nc.vector.tensor_copy(picked[:, u * S:(u + 1) * S], ds_win[:].indirect(lst[:, 16 * pair:16 * (pair + 1)]))
-            return place_scale_rows((nc.sync, nc.sync), picked, f"ds_plane{pair}")
+            return place_scale_rows(picked, f"ds_plane{pair}")
 
         ds_planes = [pick_d_scales(0, "xw")]
         dw = keep.tile([P, 2 * H], U32, align_bytes=64, tag="w1w")

from contextlib import ExitStack

import concourse.mybir as mybir

F32 = mybir.dt.float32
BF16 = mybir.dt.bfloat16
U32 = mybir.dt.uint32
I32 = mybir.dt.int32
U16 = mybir.dt.uint16
U8 = mybir.dt.uint8
FP8X4 = mybir.dt.float8_e4m3fn_x4
FP4X4 = mybir.dt.float4_e2m1fn_x4
ALU = mybir.AluOpType
COPY = mybir.ActivationFunctionType.Copy

P = 128
K, T, S, H, G, U = 512, 2048, 256, 512, 2048, 512
PACK = 4
HALF = S // 2
H_WINDOW = S + 16
FLOPS = 2 * K * H * S * 3


def tile_picked_hdaqsendmxpagmx_none_p_kernel(
    tc, x_words, x_scales, w1_words, w1_scales, gs, d_words, d_scales, offs, n1, ka, kb, n2, n3, n4, out
):
    nc = tc.nc
    with ExitStack() as ctx:
        keep = ctx.enter_context(tc.tile_pool(name="keep", bufs=1))
        psum = ctx.enter_context(tc.psum_pool(name="psum", bufs=1))

        def load_list(src, name):
            lst = keep.tile(list(src.shape), U16, name=name)
            nc.sync.dma_start(lst[:], src)
            return lst

        def load_scale_rows(queues, clear, src, name):
            window = keep.tile([P, T], U8, name=name)
            clear.memset(window[:].bitcast(I32), 0)
            rows = src[0].bitcast(I32)
            for j in range(2):
                queues[j].dma_start(window[:].bitcast(I32)[j:P:16, :], rows[j:16:2, :])
            return window

        def place_scale_rows(picked, name):
            plane = keep.tile(list(picked.shape), U8, name=name, align_bytes=64)
            nc.vector.tensor_copy(plane[:].bitcast(I32), picked[:].bitcast(I32))
            for j in range(2):
                nc.sync.dma_start(plane[:].bitcast(I32)[2 + j:P:32, :], picked[:].bitcast(I32)[16 + j:P:32, :])
            return plane

        def load_words(src, name):
            window = keep.tile([P, T], U32, name=name, tag=name, align_bytes=64)
            nc.sync.dma_start(window[:].bitcast(I32), src[0].rearrange("p c r -> p (c r)").bitcast(I32))
            return window

        offs_t = load_list(offs, "offs_t")
        w1w_raw = keep.tile([P, 2 * H], U8)
        nc.scalar.dma_start(w1w_raw[:].bitcast(I32), w1_words[0].bitcast(I32))
        xs_win = load_scale_rows((nc.sync, nc.scalar), nc.gpsimd, x_scales, "xs_win")
        w1s_raw = keep.tile([P, H], U8)
        nc.vector.memset(w1s_raw[:].bitcast(I32), 0)
        for j, queue in enumerate((nc.sync, nc.scalar, nc.scalar, nc.scalar)):
            queue.dma_start(w1s_raw[:].bitcast(I32)[j:P:32, :], w1_scales[0].bitcast(I32)[j:16:4, :])
        xw_win = load_words(x_words, "xw_win")

        xs_picked = keep.tile([P, S], U8)
        nc.vector.tensor_copy(xs_picked[:], xs_win[:].indirect(offs_t[:]))
        xs_plane = place_scale_rows(xs_picked, "xs_plane")

        w1w = keep.tile([P, 2 * H], U8, align_bytes=64, tag="w1w")
        nc.scalar.copy(
            w1w[:].bitcast(U16).rearrange("p (t m) -> p t m", t=PACK),
            w1w_raw[:].bitcast(U16).rearrange("p (m t) -> p t m", t=PACK),
        )
        w1s = keep.tile([P, H], U8, align_bytes=64)
        nc.vector.tensor_copy(
            w1s[:].rearrange("p (t m) -> p t m", t=PACK), w1s_raw[:].rearrange("p (m t) -> p t m", t=PACK)
        )
        xw = keep.tile([P, S], U32, align_bytes=64, tag="xw")
        nc.vector.tensor_copy(xw[:], xw_win[:].indirect(offs_t[:]))

        gs_t = keep.tile([P, PACK], F32)
        nc.sync.dma_start(gs_t[:], gs.rearrange("(p t) o -> p (t o)", t=PACK))
        n1_t = load_list(n1, "n1_t")
        ka_t = load_list(ka, "ka_t")
        kb_t = load_list(kb, "kb_t")
        ds_win = load_scale_rows((nc.gpsimd, nc.gpsimd), nc.vector, d_scales, "ds_win")
        dw_win = load_words(d_words, "dw_win")

        gy, gds = [], []
        for t in range(PACK):
            y_ps = psum.tile([P, S], F32, name=f"y_ps{t}", tag=f"bank{t}")
            nc.tensor.matmul_mx(
                y_ps[:], w1w[:, 2 * P * t:2 * P * (t + 1)].bitcast(FP4X4), w1s[:, P * t:P * (t + 1)],
                xw[:].bitcast(FP8X4), xs_plane[:], start=True, stop=True,
            )
            gy_t = keep.tile([P, S], F32, name=f"gy{t}")
            if t == 0:
                nc.scalar.activation(gy_t[:], y_ps[:], COPY, scale=gs_t[:, t:t + 1])
            else:
                nc.vector.tensor_scalar(gy_t[:], y_ps[:], gs_t[:, t:t + 1], None, ALU.mult)
            gds_t = keep.tile([P, 2 * S], F32, name=f"gds{t}")
            nc.scalar.activation(gds_t[:].indirect(n1_t[:]), gy_t[:], COPY)
            gy.append(gy_t)
            gds.append(gds_t)

        def pick_d_scales(pair, tag):
            picked = keep.tile([P, 2 * S], U8, name=f"ds_picked{pair}", align_bytes=64, tag=tag)
            for u, lst in enumerate((ka_t, kb_t)):
                nc.vector.tensor_copy(picked[:, u * S:(u + 1) * S], ds_win[:].indirect(lst[:, 16 * pair:16 * (pair + 1)]))
            return place_scale_rows(picked, f"ds_plane{pair}")

        ds_planes = [pick_d_scales(0, "xw")]
        dw = keep.tile([P, 2 * H], U32, align_bytes=64, tag="w1w")
        for u, lst in enumerate((ka_t, kb_t)):
            nc.vector.tensor_copy(dw[:, u * H:(u + 1) * H], dw_win[:].indirect(lst[:]))

        z_store = keep.tile([P, (2 * PACK - 1) * S], BF16, align_bytes=64, tag="dw_win")
        z = z_store[:, :PACK * S].rearrange("p (c t) -> p c t", t=PACK)
        z_planes = z_store[:, PACK * S:].rearrange("p (t c) -> p t c", c=S)
        for t in range(PACK - 1):
            nc.vector.tensor_tensor(z_planes[:, t, :], gy[t][:], gds[t][:, :S], ALU.subtract)
        nc.vector.tensor_copy(z[:, :, :PACK - 1], z_planes.rearrange("p t c -> p c t"))
        halves = [slice(0, HALF), slice(HALF, S)]
        for cols in halves:
            nc.vector.tensor_tensor(z[:, cols, 3], gy[3][:, cols], gds[3][:, cols], ALU.subtract)
        zw = keep.tile([P, S], U32, align_bytes=64)
        zs = keep.tile([P, S], U8, align_bytes=64)
        for cols in halves:
            nc.vector.quantize_mx(zw[:, cols].bitcast(FP8X4), zs[:, cols], z_store[:, PACK * cols.start:PACK * cols.stop])

        n4_t = load_list(n4, "n4_t")
        n2_t = load_list(n2, "n2_t")
        n3_t = load_list(n3, "n3_t")

        def product(m):
            h = keep.tile([P, H_WINDOW], F32, name=f"h{m}")
            nc.vector.memset(h[:, S:], 0.0)
            for i, cols in enumerate(halves if m == 0 else [slice(0, S)]):
                h_ps = psum.tile([P, cols.stop - cols.start], F32, name=f"h_ps{m}_{i}", tag=f"bank{(PACK + m + i + (m > 0)) % 8}")
                for u in range(2):
                    nc.tensor.matmul_mx(
                        h_ps[:], dw[:, u * H + m * P:u * H + (m + 1) * P].bitcast(FP8X4),
                        ds_planes[m // 2][:, u * S + (m % 2) * P:u * S + (m % 2 + 1) * P],
                        zw[:, cols].bitcast(FP8X4), zs[:, cols], start=(u == 0), stop=(u == 1),
                    )
                if m == 0:
                    nc.scalar.activation(h[:, cols], h_ps[:], COPY, scale=0.0625)
                else:
                    nc.vector.tensor_scalar(h[:, cols], h_ps[:], 0.0625, None, ALU.mult)
            return h

        def combine(m, h, other, op):
            res = keep.tile([P, S], F32, name=f"res{m}")
            nc.vector.tensor_tensor(res[:], h[:, :S], other[:], op)
            return res

        for pair in range(2):
            if pair == 1:
                ds_planes.append(pick_d_scales(1, "dw_win"))
            blocks = (2 * pair, 2 * pair + 1)
            hs = [product(m) for m in blocks]
            others = [keep.tile([P, S], F32, name=f"other{m}") for m in blocks]
            pages = [keep.tile([P, U], F32, name=f"page{m}") for m in blocks]
            for h, other in zip(hs, others):
                nc.scalar.activation(other[:], h[:].indirect(n4_t[:]), COPY)
            for op, lst in ((ALU.max, n2_t), (ALU.min, n3_t)):
                for m, h, other, page in zip(blocks, hs, others, pages):
                    nc.scalar.activation(page[:].indirect(lst[:]), combine(m, h, other, op)[:], COPY)
            for m, page in zip(blocks, pages):
                nc.sync.dma_start(out[m * P:(m + 1) * P, :], page[:])
